import numpy as np
import ml_dtypes


def mxq(x, axis, fmt="e4m3"):
    dtype, down = {"e4m3": (ml_dtypes.float8_e4m3fn, 7), "e5m2": (ml_dtypes.float8_e5m2, 14)}[fmt]
    v = np.moveaxis(np.asarray(x, np.float32).astype(ml_dtypes.bfloat16).astype(np.float64), axis, -1)
    blocks = v.reshape(v.shape[:-1] + (-1, 32))
    amax = np.abs(blocks).max(-1, keepdims=True)
    byte = np.maximum(np.where(amax > 0, np.frexp(amax)[1] - 1 + 127, 0) - down, 1)
    scale = np.exp2(byte - 127.0)
    codes = (blocks / scale).astype(np.float32).astype(dtype).astype(np.float64)
    return np.moveaxis((codes * scale).reshape(v.shape), -1, axis)


WIDE = False


def mx_kscale(k):
    if not WIDE:
        return np.ones(k)
    levels = np.array([30, -30])
    if k % 512:
        return np.exp2(np.random.permutation(np.resize(levels, k // 32))).repeat(32)
    a = np.empty((k // 512, 16))
    for p in range(k // 512):
        a[p, :8] = np.random.permutation(np.resize(levels, 8))
        for g in range(8):
            far = levels[np.abs(levels - a[p, g]) >= 10]
            a[p, g + 8] = far[np.random.randint(len(far))]
    return np.exp2(a.ravel()).repeat(32)


def f64(x):
    return np.asarray(x).astype(np.float64)


def striped(idx):
    return np.tile(np.asarray(idx).reshape(-1, 16).T, (8, 1)).astype(np.uint16)


def unstriped(offs):
    return offs[:16].T.reshape(-1).astype(np.int64)


E2M1 = np.array([0.0, 0.5, 1.0, 1.5, 2.0, 3.0, 4.0, 6.0, -0.0, -0.5, -1.0, -1.5, -2.0, -3.0, -4.0, -6.0])


def pack_weight(w, fmt):
    k, n = w.shape
    w = f64(np.asarray(w, np.float32).astype(ml_dtypes.bfloat16)).reshape(k // 32, 32, n)
    amax = np.abs(w).max(1)
    if fmt in ("e4m3", "e5m2"):
        byte = np.frexp(amax)[1] - 1 + 127 - (7 if fmt == "e4m3" else 14)
    else:
        mant, ex = np.frexp(amax / 6.0)
        byte = np.where(mant > 0.5, ex, ex - 1) + 127
    byte = np.clip(np.where(amax > 0, byte, 1), 1, 254)
    scaled = (w * np.exp2(127.0 - byte)[:, None, :]).reshape(k, n).astype(np.float32)
    by_word = np.ascontiguousarray(scaled.reshape(k // 512, 128, 4, n).transpose(0, 1, 3, 2))
    if fmt in ("e4m3", "e5m2"):
        words = by_word.astype(ml_dtypes.float8_e4m3fn if fmt == "e4m3" else ml_dtypes.float8_e5m2).view(np.uint8)
    else:
        c = by_word.astype(ml_dtypes.float4_e2m1fn).view(np.uint8) & 0xF
        words = (c[..., 0::2] | (c[..., 1::2] << 4)).reshape(k // 512, 128, 2 * n)
    return np.ascontiguousarray(words), np.ascontiguousarray(byte.astype(np.uint8).reshape(k // 512, 16, n))


def unpack_weight(words, scales, fmt):
    g, _, n = scales.shape
    words = np.ascontiguousarray(words).reshape(g, 128, n, -1)
    if fmt in ("e4m3", "e5m2"):
        vals = words.view(ml_dtypes.float8_e4m3fn if fmt == "e4m3" else ml_dtypes.float8_e5m2).astype(np.float64)
    else:
        nib = np.empty((g, 128, n, 4), np.uint8)
        nib[..., 0::2] = words & 0xF
        nib[..., 1::2] = words >> 4
        vals = E2M1[nib]
    vals = vals * np.repeat(np.exp2(scales.astype(np.float64) - 127.0), 8, axis=1)[..., None]
    return vals.transpose(0, 1, 3, 2).reshape(g * 512, n)


K, T, J, B, R, V, N, Z = 1024, 1024, 256, 32, 512, 512, 256, 512


def setup_inputs():
    n = np.random.standard_normal
    idx = np.random.permutation(T)[:J]
    idx2 = np.random.permutation(V)[:J]
    idx3 = np.random.permutation(V)[:J]
    idx4 = np.random.permutation(Z)[:J]
    fk = mx_kscale(K)
    fr = mx_kscale(R)
    wp = pack_weight(n((K, R)) * 1 / np.sqrt(K) * fk[:, None] * fr, "e2m1")
    wbp = pack_weight(n((R, N)) * 1 / np.sqrt(R) / fr[:, None], "e5m2")
    return {
        "xf": (n((K, T))).astype(np.float32),
        "fk": (np.random.uniform(0.5, 2.0, (K, 1)) / fk[:, None]).astype(np.float32),
        "w_words": wp[0],
        "w_scales": wp[1],
        "tb": (n((R, V)) * 0.7 * fr[:, None]).astype(np.float32),
        "wb_words": wbp[0],
        "wb_scales": wbp[1],
        "tz": (n((N, Z)) * 0.6).astype(np.float32),
        "rw": (np.random.uniform(0.5, 2.0, (1, J))).astype(np.float32),
        "offs": striped(idx),
        "offs2": striped(idx2),
        "offs3": striped(idx3),
        "offs4": striped(idx4),
    }


def reference(xf, fk, w_words, w_scales, tb, wb_words, wb_scales, tz, rw, offs, offs2, offs3, offs4):
    idx = unstriped(offs)
    idx2 = unstriped(offs2)
    idx3 = unstriped(offs3)
    idx4 = unstriped(offs4)
    wu = unpack_weight(w_words, w_scales, "e2m1")
    wbu = unpack_weight(wb_words, wb_scales, "e5m2")
    xg = f64(xf)[:, idx]
    g1 = xg.reshape(K, B, J // B).mean(axis=2)
    g2 = np.repeat(g1, J // B, axis=1)
    u = (xg - g2) * f64(fk)
    uq = mxq(u, 0, "e4m3")
    a = wu.T @ uq
    hid = np.maximum(a + f64(tb)[:, idx2] - f64(tb)[:, idx3], 0.0)
    hidq = mxq(hid, 0, "e5m2")
    p = wbu.T @ hidq
    y = np.maximum(p, f64(tz)[:, idx4]) * f64(rw)
    return y

@@ -1,0 +1,328 @@
+from contextlib import ExitStack
+
+import concourse.mybir as mybir
+from concourse.masks import make_identity
+
+K, T, J, R, V, N, Z = 1024, 1024, 256, 512, 512, 256, 512
+GROUP = 8
+
+F32 = mybir.dt.float32
+BF16 = mybir.dt.bfloat16
+I32 = mybir.dt.int32
+U32 = mybir.dt.uint32
+U16 = mybir.dt.uint16
+U8 = mybir.dt.uint8
+E4M3X4 = mybir.dt.float8_e4m3fn_x4
+E5M2X4 = mybir.dt.float8_e5m2_x4
+E2M1X4 = mybir.dt.float4_e2m1fn_x4
+ALU = mybir.AluOpType
+COPY = mybir.ActivationFunctionType.Copy
+
+P = 128
+PACK = 4
+PASSES = K // (P * PACK)
+HALVES = 2
+JH = J // HALVES
+LIST_COLS = J // 16
+NT = N // P
+
+FLOPS = 2 * K * R * J + 2 * R * N * J
+
+
+def tile_list_centredpicks_tworeach_floored_kernel(
+    tc, xf, fk, w_words, w_scales, tb, wb_words, wb_scales, tz, rw, offs, offs2, offs3, offs4, out
+):
+    nc = tc.nc
+    with ExitStack() as ctx:
+        sb = ctx.enter_context(tc.tile_pool(name="sb", bufs=1))
+        ps = ctx.enter_context(tc.psum_pool(name="ps", bufs=1))
+
+        def tile(name, shape, dtype):
+            return sb.tile(shape, dtype, name=name, align_bytes=64)
+
+        list_x = tile("list_x", [P, LIST_COLS], U16)
+        list_add = tile("list_add", [P, LIST_COLS], U16)
+        list_sub = tile("list_sub", [P, LIST_COLS], U16)
+        list_z = tile("list_z", [P, LIST_COLS], U16)
+        x_plane = [[tile("x_%d_%d" % (a, t), [P, T], F32) for t in range(PACK)] for a in range(PASSES)]
+        tb_plane = [tile("tb_%d" % t, [P, V], F32) for t in range(PACK)]
+        tz_rows = [tile("tz_%d" % c, [P, Z], F32) for c in range(NT)]
+        fk_cols = tile("fk_cols", [P, PASSES, PACK], F32)
+        rw_pairs = tile("rw_pairs", [P, 2], F32)
+        w_raw = tile("w_raw", [P, PASSES, 2 * R], U8)
+        w_scale_raw = tile("w_scale_raw", [P, PASSES, R], U8)
+        w_codes = tile("w_codes", [P, PASSES, 2 * R], U8)
+        w_scale = tile("w_scale", [P, PASSES, R], U8)
+        wb_codes = tile("wb_codes", [P, N], U32)
+        wb_scale = tile("wb_scale", [P, N], U8)
+        ident = tile("ident", [P, P], F32)
+
+        nc.gpsimd.memset(w_scale_raw[:].bitcast(U32), 0)
+        nc.gpsimd.memset(wb_scale[:].bitcast(U32), 0)
+        make_identity(nc, ident[:])
+
+        x_rows = xf.rearrange("(a p t) c -> a t p c", p=P, t=PACK)
+        tb_rows = tb.rearrange("(p t) c -> t p c", t=PACK)
+
+        def load_x(i):
+            a, t = divmod(i, PACK)
+            nc.sync.dma_start(x_plane[a][t][:], x_rows[a, t])
+
+        def load_tb(t):
+            nc.sync.dma_start(tb_plane[t][:], tb_rows[t])
+
+        def load_w_scale(q):
+            nc.sync.dma_start(
+                w_scale_raw[32 * q : 32 * q + 4].bitcast(I32),
+                w_scales[:, 4 * q : 4 * q + 4, :].rearrange("a r c -> r a c").bitcast(I32),
+            )
+
+        def load_wb_scale(q):
+            nc.sync.dma_start(wb_scale[32 * q : 32 * q + 4].bitcast(I32), wb_scales[0, 4 * q : 4 * q + 4, :].bitcast(I32))
+
+        nc.sync.dma_start(list_x[:], offs)
+        load_x(0)
+        nc.sync.dma_start(fk_cols[:], fk.rearrange("(a p t) o -> p a (t o)", p=P, t=PACK))
+        load_x(1)
+        nc.sync.dma_start(list_add[:], offs2)
+        nc.sync.dma_start(list_sub[:], offs3)
+        load_tb(0)
+        load_x(2)
+        nc.sync.dma_start(w_raw[:].bitcast(I32), w_words.rearrange("a p c -> p a c").bitcast(I32))
+        load_w_scale(0)
+        load_w_scale(1)
+        load_x(3)
+        load_w_scale(2)
+        load_w_scale(3)
+        load_tb(1)
+        load_x(4)
+        nc.sync.dma_start(rw_pairs[:], rw.rearrange("o (p e) -> p (o e)", e=2))
+        load_wb_scale(0)
+        load_x(5)
+        load_wb_scale(1)
+        load_wb_scale(2)
+        load_x(6)
+        load_wb_scale(3)
+        nc.sync.dma_start(list_z[:], offs4)
+        load_x(7)
+        load_tb(2)
+        load_tb(3)
+        nc.sync.dma_start(wb_codes[:].bitcast(I32), wb_words[0].rearrange("p n t -> p (n t)").bitcast(I32))
+        for c in range(NT):
+            nc.sync.dma_start(tz_rows[c][:], tz[c * P : (c + 1) * P, :])
+
+        def gather(dst, window, offsets, h0, h1):
+            nc.scalar.activation(
+                dst[:, h0 * JH : h1 * JH],
+                window[:].indirect(offsets[:, h0 * LIST_COLS // HALVES : h1 * LIST_COLS // HALVES]),
+                COPY,
+            )
+
+        def gather_on_vector(dst, window, offsets, h0, h1):
+            nc.vector.tensor_copy(
+                dst[:, h0 * JH : h1 * JH],
+                window[:].indirect(offsets[:, h0 * LIST_COLS // HALVES : h1 * LIST_COLS // HALVES]),
+            )
+
+        picked = [[tile("picked_%d_%d" % (a, t), [P, J], F32) for t in range(PACK)] for a in range(PASSES)]
+        sums = [[tile("sums_%d_%d" % (a, t), [P, J // GROUP], F32) for t in range(PACK)] for a in range(PASSES)]
+        means = [[tile("means_%d_%d" % (a, t), [P, J // GROUP], F32) for t in range(PACK)] for a in range(PASSES)]
+        u_planes = [tile("u_planes_%d" % a, [P, HALVES, PACK, JH], BF16) for a in range(PASSES)]
+        u_woven = [tile("u_woven_%d" % a, [P, J, PACK], BF16) for a in range(PASSES)]
+        u_codes = [tile("u_codes_%d" % a, [P, J], U32) for a in range(PASSES)]
+        u_scale = [tile("u_scale_%d" % a, [P, J], U8) for a in range(PASSES)]
+        tb_add = [tile("tb_add_%d" % t, [P, J], F32) for t in range(PACK)]
+        tb_sub = [tile("tb_sub_%d" % t, [P, J], F32) for t in range(PACK)]
+        tb_diff = tile("tb_diff", [P, HALVES, PACK, JH], F32)
+        a_acc = [ps.tile([P, PACK, JH], F32, name="a_acc_%d" % h) for h in range(HALVES)]
+        p_acc = [ps.tile([P, NT, JH], F32, name="p_acc_%d" % h) for h in range(HALVES)]
+        rw_all = ps.tile([P, 2, P], F32, name="rw_all")
+        BH = JH // GROUP
+
+        def group_sums(a, t, h0, h1):
+            nc.vector.tensor_reduce(
+                sums[a][t][:, h0 * BH : h1 * BH],
+                picked[a][t][:, h0 * JH : h1 * JH].rearrange("p (b i) -> p b i", i=GROUP),
+                mybir.AxisListType.X,
+                ALU.add,
+            )
+
+        def group_means(a, t, h0, h1):
+            nc.vector.tensor_scalar(
+                means[a][t][:, h0 * BH : h1 * BH],
+                sums[a][t][:, h0 * BH : h1 * BH],
+                fk_cols[:, a, t : t + 1],
+                1.0 / GROUP,
+                ALU.mult,
+                ALU.mult,
+            )
+
+        def centre(a, t, h0, h1):
+            nh = h1 - h0
+            nc.vector.scalar_tensor_tensor(
+                u_planes[a][:, h0:h1, t, :].rearrange("p h (b i) -> p h b i", i=GROUP),
+                picked[a][t][:, h0 * JH : h1 * JH].rearrange("p (h b i) -> p h b i", h=nh, i=GROUP),
+                fk_cols[:, a, t : t + 1],
+                means[a][t][:, h0 * BH : h1 * BH]
+                .rearrange("p (h b) -> p h b", h=nh)
+                .unsqueeze(3)
+                .to_broadcast([P, nh, BH, GROUP]),
+                ALU.mult,
+                ALU.subtract,
+            )
+
+        def weave_u(a, h):
+            nc.vector.tensor_copy(
+                u_woven[a][:, h * JH : (h + 1) * JH, :].rearrange("p (c i) t -> p c t i", i=4),
+                u_planes[a][:, h].rearrange("p t (c i) -> p c t i", i=4),
+            )
+
+        def quantise_u(a, h):
+            cols = slice(h * JH, (h + 1) * JH)
+            nc.vector.quantize_mx(
+                out=u_codes[a][:, cols].bitcast(E4M3X4),
+                scales=u_scale[a][:, cols],
+                in_=u_woven[a][:, cols, :].rearrange("p j t -> p (j t)"),
+            )
+
+        def first_product(a, h):
+            cols = slice(h * JH, (h + 1) * JH)
+            for t in range(PACK):
+                nc.tensor.matmul_mx(
+                    out=a_acc[h][:, t, :],
+                    lhsT=w_codes[:, a, 2 * P * t : 2 * P * (t + 1)].bitcast(E2M1X4),
+                    lhsT_scale=w_scale[:, a, P * t : P * (t + 1)],
+                    rhs=u_codes[a][:, cols].bitcast(E4M3X4),
+                    rhs_scale=u_scale[a][:, cols],
+                    start=(a == 0 and t == 0),
+                    stop=(a == PASSES - 1 and t == PACK - 1),
+                )
+
+        def table_difference(t, h0, h1):
+            cols = slice(h0 * JH, h1 * JH)
+            nc.vector.tensor_tensor(
+                tb_diff[:, h0:h1, t, :],
+                tb_add[t][:, cols].rearrange("p (h j) -> p h j", j=JH),
+                tb_sub[t][:, cols].rearrange("p (h j) -> p h j", j=JH),
+                ALU.subtract,
+            )
+
+        def x_whole(i, gather=gather):
+            a, t = divmod(i, PACK)
+            gather(picked[a][t], x_plane[a][t], list_x, 0, HALVES)
+            group_sums(a, t, 0, HALVES)
+            group_means(a, t, 0, HALVES)
+            centre(a, t, 0, HALVES)
+
+        def tb_whole(t):
+            gather(tb_add[t], tb_plane[t], list_add, 0, HALVES)
+            gather(tb_sub[t], tb_plane[t], list_sub, 0, HALVES)
+            table_difference(t, 0, HALVES)
+
+        x_whole(0, gather_on_vector)
+        x_whole(1)
+        tb_whole(0)
+        x_whole(2)
+        nc.vector.tensor_copy(
+            w_codes[:].bitcast(U16).rearrange("p a (t b i) -> p a b t i", t=PACK, i=8),
+            w_raw[:].bitcast(U16).rearrange("p a (b i t) -> p a b t i", t=PACK, i=8),
+        )
+        x_whole(3)
+        nc.vector.tensor_copy(
+            w_scale[:].rearrange("p a (t b i) -> p a b t i", t=PACK, i=16),
+            w_scale_raw[:].rearrange("p a (b i t) -> p a b t i", t=PACK, i=16),
+        )
+        for h in range(HALVES):
+            weave_u(0, h)
+        for h in range(HALVES):
+            quantise_u(0, h)
+        for h in range(HALVES):
+            first_product(0, h)
+        tb_whole(1)
+        x_whole(4)
+        for e in range(2):
+            nc.tensor.transpose(rw_all[:, e, :], rw_pairs[:, e : e + 1].to_broadcast([P, P]), ident[:])
+        x_whole(5)
+        x_whole(6)
+
+        last = (PASSES - 1, PACK - 1)
+        gather_on_vector(picked[last[0]][last[1]], x_plane[last[0]][last[1]], list_x, 0, 1)
+        gather(picked[last[0]][last[1]], x_plane[last[0]][last[1]], list_x, 1, 2)
+        for step in (group_sums, group_means, centre):
+            for h in range(HALVES):
+                step(last[0], last[1], h, h + 1)
+        for step in (weave_u, quantise_u, first_product):
+            for h in range(HALVES):
+                step(last[0], h)
+        for h in range(HALVES):
+            for t in (2, 3):
+                gather(tb_add[t], tb_plane[t], list_add, h, h + 1)
+                gather(tb_sub[t], tb_plane[t], list_sub, h, h + 1)
+                table_difference(t, h, h + 1)
+
+        z_picked = [tile("z_picked_%d" % h, [P, NT, JH], F32) for h in range(HALVES)]
+        for h in range(HALVES):
+            for c in range(NT):
+                nc.scalar.activation(
+                    z_picked[h][:, c, :],
+                    tz_rows[c][:].indirect(list_z[:, h * LIST_COLS // HALVES : (h + 1) * LIST_COLS // HALVES]),
+                    COPY,
+                )
+
+        pre = [tile("pre_%d" % h, [P, PACK, JH], BF16) for h in range(HALVES)]
+        hid_woven = [tile("hid_woven_%d" % h, [P, JH, PACK], BF16) for h in range(HALVES)]
+        hid_codes = [tile("hid_codes_%d" % h, [P, JH], U32) for h in range(HALVES)]
+        hid_scale = [tile("hid_scale_%d" % h, [P, JH], U8) for h in range(HALVES)]
+        floored = [tile("floored_%d" % h, [P, NT, JH], F32) for h in range(HALVES)]
+        result = [tile("result_%d" % h, [P, NT, JH], F32) for h in range(HALVES)]
+        out_rows = out.rearrange("(c p) j -> p c j", p=P)
+
+        def add_table(h):
+            nc.vector.tensor_tensor(pre[h][:], a_acc[h][:], tb_diff[:, h], ALU.add)
+
+        def relu_weave(h):
+            nc.vector.tensor_scalar(
+                hid_woven[h][:].rearrange("p (c i) t -> p c t i", i=4),
+                pre[h][:].rearrange("p t (c i) -> p c t i", i=4),
+                0.0,
+                None,
+                ALU.max,
+            )
+
+        def quantise_hid(h):
+            nc.vector.quantize_mx(
+                out=hid_codes[h][:].bitcast(E5M2X4),
+                scales=hid_scale[h][:],
+                in_=hid_woven[h][:].rearrange("p j t -> p (j t)"),
+            )
+
+        def second_product(h):
+            for c in range(NT):
+                nc.tensor.matmul_mx(
+                    out=p_acc[h][:, c, :],
+                    lhsT=wb_codes[:, c * P : (c + 1) * P].bitcast(E5M2X4),
+                    lhsT_scale=wb_scale[:, c * P : (c + 1) * P],
+                    rhs=hid_codes[h][:].bitcast(E5M2X4),
+                    rhs_scale=hid_scale[h][:],
+                    start=True,
+                    stop=True,
+                )
+
+        def floor_by_table(h):
+            nc.vector.tensor_tensor(floored[h][:], p_acc[h][:], z_picked[h][:], ALU.max)
+
+        def weigh(h):
+            half_pairs = slice(h * JH // 2, (h + 1) * JH // 2)
+            nc.vector.tensor_tensor(
+                result[h][:].rearrange("p c (m e) -> p c m e", e=2),
+                floored[h][:].rearrange("p c (m e) -> p c m e", e=2),
+                rw_all[:, :, half_pairs].rearrange("p e m -> p m e").unsqueeze(1).to_broadcast([P, NT, JH // 2, 2]),
+                ALU.mult,
+            )
+
+        def store(h):
+            nc.sync.dma_start(out_rows[:, :, h * JH : (h + 1) * JH], result[h][:])
+
+        for step in (add_table, relu_weave, quantise_hid, second_product, floor_by_table, weigh, store):
+            for h in range(HALVES):
+                step(h)

@@ -47,7 +47,8 @@ def tile_list_centredpicks_tworeach_floored_kernel(
         x_plane = [[tile("x_%d_%d" % (a, t), [P, T], F32) for t in range(PACK)] for a in range(PASSES)]
         tb_plane = [tile("tb_%d" % t, [P, V], F32) for t in range(PACK)]
         tz_rows = [tile("tz_%d" % c, [P, Z], F32) for c in range(NT)]
-        fk_cols = tile("fk_cols", [P, PASSES, PACK], F32)
+        fk_padded = tile("fk_padded", [P, PASSES, 2 * PACK], F32)
+        fk_cols = fk_padded[:, :, :PACK]
         rw_pairs = tile("rw_pairs", [P, 2], F32)
         w_raw = tile("w_raw", [P, PASSES, 2 * R], U8)
         w_scale_raw = tile("w_scale_raw", [P, PASSES, R], U8)
@@ -57,9 +58,11 @@ def tile_list_centredpicks_tworeach_floored_kernel(
         wb_scale = tile("wb_scale", [P, N], U8)
         ident = tile("ident", [P, P], F32)
 
-        nc.gpsimd.memset(w_scale_raw[:].bitcast(U32), 0)
-        nc.gpsimd.memset(wb_scale[:].bitcast(U32), 0)
-        make_identity(nc, ident[:])
+        nc.vector.memset(w_scale_raw[:].bitcast(U32), 0)
+        nc.vector.memset(wb_scale[:].bitcast(U32), 0)
+        warm = tile("warm", [P, 2], F32)
+        nc.vector.memset(warm[:, 0:1], 0.0)
+        nc.scalar.activation(warm[:, 1:2], warm[:, 0:1], COPY)
 
         x_rows = xf.rearrange("(a p t) c -> a t p c", p=P, t=PACK)
         tb_rows = tb.rearrange("(p t) c -> t p c", t=PACK)
@@ -71,8 +74,8 @@ def tile_list_centredpicks_tworeach_floored_kernel(
         def load_tb(t):
             nc.sync.dma_start(tb_plane[t][:], tb_rows[t])
 
-        def load_w_scale(q):
-            nc.sync.dma_start(
+        def load_w_scale(q, queue=nc.sync):
+            queue.dma_start(
                 w_scale_raw[32 * q : 32 * q + 4].bitcast(I32),
                 w_scales[:, 4 * q : 4 * q + 4, :].rearrange("a r c -> r a c").bitcast(I32),
             )
@@ -80,36 +83,37 @@ def tile_list_centredpicks_tworeach_floored_kernel(
         def load_wb_scale(q):
             nc.sync.dma_start(wb_scale[32 * q : 32 * q + 4].bitcast(I32), wb_scales[0, 4 * q : 4 * q + 4, :].bitcast(I32))
 
+        load_w_scale(0, nc.gpsimd)
+        load_w_scale(1, nc.gpsimd)
+        make_identity(nc, ident[:])
         nc.sync.dma_start(list_x[:], offs)
         load_x(0)
-        nc.sync.dma_start(fk_cols[:], fk.rearrange("(a p t) o -> p a (t o)", p=P, t=PACK))
-        load_x(1)
         nc.sync.dma_start(list_add[:], offs2)
         nc.sync.dma_start(list_sub[:], offs3)
-        load_tb(0)
+        load_tb(3)
+        nc.sync.dma_start(fk_cols[:], fk.rearrange("(a p t) o -> p a (t o)", p=P, t=PACK))
+        load_x(1)
         load_x(2)
-        nc.sync.dma_start(w_raw[:].bitcast(I32), w_words.rearrange("a p c -> p a c").bitcast(I32))
-        load_w_scale(0)
-        load_w_scale(1)
-        load_x(3)
         load_w_scale(2)
         load_w_scale(3)
-        load_tb(1)
+        load_x(3)
         load_x(4)
-        nc.sync.dma_start(rw_pairs[:], rw.rearrange("o (p e) -> p (o e)", e=2))
-        load_wb_scale(0)
         load_x(5)
+        load_x(6)
+        load_tb(0)
+        nc.sync.dma_start(w_raw[:].bitcast(I32), w_words.rearrange("a p c -> p a c").bitcast(I32))
+        load_x(7)
+        load_tb(1)
+        load_tb(2)
+        nc.sync.dma_start(list_z[:], offs4)
+        nc.sync.dma_start(rw_pairs[:], rw.rearrange("o (p e) -> p (o e)", e=2))
+        nc.sync.dma_start(tz_rows[0][:], tz[0 * P : (0 + 1) * P, :])
+        nc.sync.dma_start(tz_rows[1][:], tz[1 * P : (1 + 1) * P, :])
+        nc.sync.dma_start(wb_codes[:].bitcast(I32), wb_words[0].rearrange("p n t -> p (n t)").bitcast(I32))
+        load_wb_scale(0)
         load_wb_scale(1)
         load_wb_scale(2)
-        load_x(6)
         load_wb_scale(3)
-        nc.sync.dma_start(list_z[:], offs4)
-        load_x(7)
-        load_tb(2)
-        load_tb(3)
-        nc.sync.dma_start(wb_codes[:].bitcast(I32), wb_words[0].rearrange("p n t -> p (n t)").bitcast(I32))
-        for c in range(NT):
-            nc.sync.dma_start(tz_rows[c][:], tz[c * P : (c + 1) * P, :])
 
         def gather(dst, window, offsets, h0, h1):
             nc.scalar.activation(
@@ -124,16 +128,26 @@ def tile_list_centredpicks_tworeach_floored_kernel(
                 window[:].indirect(offsets[:, h0 * LIST_COLS // HALVES : h1 * LIST_COLS // HALVES]),
             )
 
-        picked = [[tile("picked_%d_%d" % (a, t), [P, J], F32) for t in range(PACK)] for a in range(PASSES)]
-        sums = [[tile("sums_%d_%d" % (a, t), [P, J // GROUP], F32) for t in range(PACK)] for a in range(PASSES)]
-        means = [[tile("means_%d_%d" % (a, t), [P, J // GROUP], F32) for t in range(PACK)] for a in range(PASSES)]
-        u_planes = [tile("u_planes_%d" % a, [P, HALVES, PACK, JH], BF16) for a in range(PASSES)]
-        u_woven = [tile("u_woven_%d" % a, [P, J, PACK], BF16) for a in range(PASSES)]
+        tb_diff = tile("tb_diff", [P, PACK, J], F32)
+        picked = [
+            [tb_diff[:, 3, :], tile("picked_0_1", [P, J], F32), tile("picked_0_2", [P, J], F32), tile("picked_0_3", [P, J], F32)],
+            [tile("picked_1_0", [P, J], F32), tile("picked_1_1", [P, J], F32), tile("picked_1_2", [P, J], F32), tb_diff[:, 0, :]],
+        ]
+        means = [tile("means_%d" % a, [P, PACK, J // GROUP], F32) for a in range(PASSES)]
+        u_planes = [
+            tile("u_planes_0", [P, HALVES, PACK, JH], BF16),
+            tb_diff[:, 1:3, :].bitcast(BF16).rearrange("p h (t j) -> p h t j", j=JH),
+        ]
+        spent = u_planes[0][:, HALVES - 1].bitcast(F32)
+        sums = [
+            [tile("sums_0_%d" % t, [P, J // GROUP], F32) for t in range(PACK)],
+            [tile("sums_1_%d" % t, [P, J // GROUP], F32) for t in range(PACK)],
+        ]
+        u_woven = [tile("u_woven_%d" % a, [P, HALVES, JH, PACK], BF16) for a in range(PASSES)]
         u_codes = [tile("u_codes_%d" % a, [P, J], U32) for a in range(PASSES)]
         u_scale = [tile("u_scale_%d" % a, [P, J], U8) for a in range(PASSES)]
         tb_add = [tile("tb_add_%d" % t, [P, J], F32) for t in range(PACK)]
         tb_sub = [tile("tb_sub_%d" % t, [P, J], F32) for t in range(PACK)]
-        tb_diff = tile("tb_diff", [P, HALVES, PACK, JH], F32)
         a_acc = [ps.tile([P, PACK, JH], F32, name="a_acc_%d" % h) for h in range(HALVES)]
         p_acc = [ps.tile([P, NT, JH], F32, name="p_acc_%d" % h) for h in range(HALVES)]
         rw_all = ps.tile([P, 2, P], F32, name="rw_all")
@@ -149,7 +163,7 @@ def tile_list_centredpicks_tworeach_floored_kernel(
 
         def group_means(a, t, h0, h1):
             nc.vector.tensor_scalar(
-                means[a][t][:, h0 * BH : h1 * BH],
+                means[a][:, t, h0 * BH : h1 * BH],
                 sums[a][t][:, h0 * BH : h1 * BH],
                 fk_cols[:, a, t : t + 1],
                 1.0 / GROUP,
@@ -163,7 +177,7 @@ def tile_list_centredpicks_tworeach_floored_kernel(
                 u_planes[a][:, h0:h1, t, :].rearrange("p h (b i) -> p h b i", i=GROUP),
                 picked[a][t][:, h0 * JH : h1 * JH].rearrange("p (h b i) -> p h b i", h=nh, i=GROUP),
                 fk_cols[:, a, t : t + 1],
-                means[a][t][:, h0 * BH : h1 * BH]
+                means[a][:, t, h0 * BH : h1 * BH]
                 .rearrange("p (h b) -> p h b", h=nh)
                 .unsqueeze(3)
                 .to_broadcast([P, nh, BH, GROUP]),
@@ -171,9 +185,9 @@ def tile_list_centredpicks_tworeach_floored_kernel(
                 ALU.subtract,
             )
 
-        def weave_u(a, h):
-            nc.vector.tensor_copy(
-                u_woven[a][:, h * JH : (h + 1) * JH, :].rearrange("p (c i) t -> p c t i", i=4),
+        def weave_u(a, h, copy=nc.vector.tensor_copy):
+            copy(
+                u_woven[a][:, h].rearrange("p (c i) t -> p c t i", i=4),
                 u_planes[a][:, h].rearrange("p t (c i) -> p c t i", i=4),
             )
 
@@ -182,7 +196,7 @@ def tile_list_centredpicks_tworeach_floored_kernel(
             nc.vector.quantize_mx(
                 out=u_codes[a][:, cols].bitcast(E4M3X4),
                 scales=u_scale[a][:, cols],
-                in_=u_woven[a][:, cols, :].rearrange("p j t -> p (j t)"),
+                in_=u_woven[a][:, h].rearrange("p j t -> p (j t)"),
             )
 
         def first_product(a, h):
@@ -201,65 +215,90 @@ def tile_list_centredpicks_tworeach_floored_kernel(
         def table_difference(t, h0, h1):
             cols = slice(h0 * JH, h1 * JH)
             nc.vector.tensor_tensor(
-                tb_diff[:, h0:h1, t, :],
-                tb_add[t][:, cols].rearrange("p (h j) -> p h j", j=JH),
-                tb_sub[t][:, cols].rearrange("p (h j) -> p h j", j=JH),
+                tb_diff[:, t, cols],
+                tb_add[t][:, cols],
+                tb_sub[t][:, cols],
                 ALU.subtract,
             )
 
-        def x_whole(i, gather=gather):
-            a, t = divmod(i, PACK)
+        def pick_and_sum(a, t, gather=gather):
             gather(picked[a][t], x_plane[a][t], list_x, 0, HALVES)
             group_sums(a, t, 0, HALVES)
-            group_means(a, t, 0, HALVES)
-            centre(a, t, 0, HALVES)
 
         def tb_whole(t):
             gather(tb_add[t], tb_plane[t], list_add, 0, HALVES)
             gather(tb_sub[t], tb_plane[t], list_sub, 0, HALVES)
             table_difference(t, 0, HALVES)
 
-        x_whole(0, gather_on_vector)
-        x_whole(1)
-        tb_whole(0)
-        x_whole(2)
-        nc.vector.tensor_copy(
-            w_codes[:].bitcast(U16).rearrange("p a (t b i) -> p a b t i", t=PACK, i=8),
-            w_raw[:].bitcast(U16).rearrange("p a (b i t) -> p a b t i", t=PACK, i=8),
-        )
-        x_whole(3)
-        nc.vector.tensor_copy(
-            w_scale[:].rearrange("p a (t b i) -> p a b t i", t=PACK, i=16),
-            w_scale_raw[:].rearrange("p a (b i t) -> p a b t i", t=PACK, i=16),
-        )
-        for h in range(HALVES):
-            weave_u(0, h)
+        def x_whole(a, t, gather=gather):
+            pick_and_sum(a, t, gather)
+            group_means(a, t, 0, HALVES)
+            centre(a, t, 0, HALVES)
+
+        x_whole(0, 0)
+        fk_last = tile("fk_last", [P, JH], F32)
+        nc.vector.tensor_copy(fk_last[:], fk_cols[:, PASSES - 1, PACK - 1 : PACK].to_broadcast([P, JH]))
+        x_whole(0, 1)
+        gather(tb_add[3], tb_plane[3], list_add, 0, HALVES)
+        gather(tb_sub[3], tb_plane[3], list_sub, 0, HALVES)
+        table_difference(3, 0, HALVES)
+        for a in range(PASSES):
+            nc.vector.tensor_copy(
+                w_scale[:, a].rearrange("p (t b i) -> p b t i", t=PACK, i=16),
+                w_scale_raw[:, a].rearrange("p (b i t) -> p b t i", t=PACK, i=16),
+            )
+        x_whole(0, 2)
+        x_whole(0, 3)
+        weave_u(0, 0)
+        weave_u(0, 1, nc.scalar.copy)
         for h in range(HALVES):
             quantise_u(0, h)
+        x_whole(1, 0)
+        x_whole(1, 1)
+        x_whole(1, 2)
+        gather(tb_add[0], tb_plane[0], list_add, 0, HALVES)
+        gather(tb_sub[0], tb_plane[0], list_sub, 0, HALVES)
+        nc.vector.tensor_copy(
+            w_codes[:, 0:1].bitcast(U16).rearrange("p a (t b i) -> p a b t i", t=PACK, i=8),
+            w_raw[:, 0:1].bitcast(U16).rearrange("p a (b i t) -> p a b t i", t=PACK, i=8),
+        )
+        nc.vector.tensor_copy(
+            w_codes[:, 1:2].bitcast(U16).rearrange("p a (t b i) -> p a b t i", t=PACK, i=8),
+            w_raw[:, 1:2].bitcast(U16).rearrange("p a (b i t) -> p a b t i", t=PACK, i=8),
+        )
         for h in range(HALVES):
             first_product(0, h)
-        tb_whole(1)
-        x_whole(4)
-        for e in range(2):
-            nc.tensor.transpose(rw_all[:, e, :], rw_pairs[:, e : e + 1].to_broadcast([P, P]), ident[:])
-        x_whole(5)
-        x_whole(6)
-
-        last = (PASSES - 1, PACK - 1)
-        gather_on_vector(picked[last[0]][last[1]], x_plane[last[0]][last[1]], list_x, 0, 1)
-        gather(picked[last[0]][last[1]], x_plane[last[0]][last[1]], list_x, 1, 2)
-        for step in (group_sums, group_means, centre):
-            for h in range(HALVES):
-                step(last[0], last[1], h, h + 1)
-        for step in (weave_u, quantise_u, first_product):
-            for h in range(HALVES):
-                step(last[0], h)
+        a, t = PASSES - 1, PACK - 1
+        nc.vector.tensor_tensor(
+            picked[a][t][:, :JH], x_plane[a][t][:].indirect(list_x[:, : LIST_COLS // HALVES]), fk_last[:], ALU.mult
+        )
+        gather(picked[a][t], x_plane[a][t], list_x, 1, 2)
         for h in range(HALVES):
-            for t in (2, 3):
+            group_sums(a, t, h, h + 1)
+        nc.vector.scalar_tensor_tensor(
+            u_planes[a][:, 0, t, :].rearrange("p (b i) -> p b i", i=GROUP),
+            sums[a][t][:, :BH].unsqueeze(2).to_broadcast([P, BH, GROUP]),
+            -1.0 / GROUP,
+            picked[a][t][:, :JH].rearrange("p (b i) -> p b i", i=GROUP),
+            ALU.mult,
+            ALU.add,
+        )
+        group_means(a, t, 1, 2)
+        centre(a, t, 1, 2)
+        for step in (weave_u, quantise_u):
+            for h in range(HALVES):
+                step(a, h)
+        for h in range(HALVES):
+            first_product(a, h)
+        table_difference(0, 0, HALVES)
+        for h in range(HALVES):
+            for t in (1, 2):
                 gather(tb_add[t], tb_plane[t], list_add, h, h + 1)
                 gather(tb_sub[t], tb_plane[t], list_sub, h, h + 1)
                 table_difference(t, h, h + 1)
 
+        for e in range(2):
+            nc.tensor.transpose(rw_all[:, e, :], rw_pairs[:, e : e + 1].to_broadcast([P, P]), ident[:])
         z_picked = [tile("z_picked_%d" % h, [P, NT, JH], F32) for h in range(HALVES)]
         for h in range(HALVES):
             for c in range(NT):
@@ -269,7 +308,7 @@ def tile_list_centredpicks_tworeach_floored_kernel(
                     COPY,
                 )
 
-        pre = [tile("pre_%d" % h, [P, PACK, JH], BF16) for h in range(HALVES)]
+        pre = [tile("pre_%d" % h, [P, JH, PACK], BF16) for h in range(HALVES)]
         hid_woven = [tile("hid_woven_%d" % h, [P, JH, PACK], BF16) for h in range(HALVES)]
         hid_codes = [tile("hid_codes_%d" % h, [P, JH], U32) for h in range(HALVES)]
         hid_scale = [tile("hid_scale_%d" % h, [P, JH], U8) for h in range(HALVES)]
@@ -278,12 +317,17 @@ def tile_list_centredpicks_tworeach_floored_kernel(
         out_rows = out.rearrange("(c p) j -> p c j", p=P)
 
         def add_table(h):
-            nc.vector.tensor_tensor(pre[h][:], a_acc[h][:], tb_diff[:, h], ALU.add)
+            nc.vector.tensor_tensor(
+                pre[h][:].rearrange("p (c i) t -> p c t i", i=4),
+                a_acc[h][:].rearrange("p t (c i) -> p c t i", i=4),
+                tb_diff[:, :, h * JH : (h + 1) * JH].rearrange("p t (c i) -> p c t i", i=4),
+                ALU.add,
+            )
 
         def relu_weave(h):
             nc.vector.tensor_scalar(
-                hid_woven[h][:].rearrange("p (c i) t -> p c t i", i=4),
-                pre[h][:].rearrange("p t (c i) -> p c t i", i=4),
+                hid_woven[h][:],
+                pre[h][:],
                 0.0,
                 None,
                 ALU.max,

@@ -62,7 +62,6 @@ def tile_list_centredpicks_tworeach_floored_kernel(
         nc.vector.memset(wb_scale[:].bitcast(U32), 0)
         warm = tile("warm", [P, 2], F32)
         nc.vector.memset(warm[:, 0:1], 0.0)
-        nc.scalar.activation(warm[:, 1:2], warm[:, 0:1], COPY)
 
         x_rows = xf.rearrange("(a p t) c -> a t p c", p=P, t=PACK)
         tb_rows = tb.rearrange("(p t) c -> t p c", t=PACK)
@@ -83,11 +82,11 @@ def tile_list_centredpicks_tworeach_floored_kernel(
         def load_wb_scale(q):
             nc.sync.dma_start(wb_scale[32 * q : 32 * q + 4].bitcast(I32), wb_scales[0, 4 * q : 4 * q + 4, :].bitcast(I32))
 
+        load_x(0)
         load_w_scale(0, nc.gpsimd)
         load_w_scale(1, nc.gpsimd)
         make_identity(nc, ident[:])
         nc.sync.dma_start(list_x[:], offs)
-        load_x(0)
         nc.sync.dma_start(list_add[:], offs2)
         nc.sync.dma_start(list_sub[:], offs3)
         load_tb(3)
@@ -114,6 +113,8 @@ def tile_list_centredpicks_tworeach_floored_kernel(
         load_wb_scale(1)
         load_wb_scale(2)
         load_wb_scale(3)
+
+        nc.scalar.activation(warm[:, 1:2], warm[:, 0:1], COPY)
 
         def gather(dst, window, offsets, h0, h1):
             nc.scalar.activation(
@@ -149,7 +150,7 @@ def tile_list_centredpicks_tworeach_floored_kernel(
         tb_add = [tile("tb_add_%d" % t, [P, J], F32) for t in range(PACK)]
         tb_sub = [tile("tb_sub_%d" % t, [P, J], F32) for t in range(PACK)]
         a_acc = [ps.tile([P, PACK, JH], F32, name="a_acc_%d" % h) for h in range(HALVES)]
-        p_acc = [ps.tile([P, NT, JH], F32, name="p_acc_%d" % h) for h in range(HALVES)]
+        p_acc = [ps.tile([P, HALVES, JH], F32, name="p_acc_%d" % c) for c in range(NT)]
         rw_all = ps.tile([P, 2, P], F32, name="rw_all")
         BH = JH // GROUP
 
@@ -290,8 +291,8 @@ def tile_list_centredpicks_tworeach_floored_kernel(
                 step(a, h)
         for h in range(HALVES):
             first_product(a, h)
-        table_difference(0, 0, HALVES)
         for h in range(HALVES):
+            table_difference(0, h, h + 1)
             for t in (1, 2):
                 gather(tb_add[t], tb_plane[t], list_add, h, h + 1)
                 gather(tb_sub[t], tb_plane[t], list_sub, h, h + 1)
@@ -299,22 +300,16 @@ def tile_list_centredpicks_tworeach_floored_kernel(
 
         for e in range(2):
             nc.tensor.transpose(rw_all[:, e, :], rw_pairs[:, e : e + 1].to_broadcast([P, P]), ident[:])
-        z_picked = [tile("z_picked_%d" % h, [P, NT, JH], F32) for h in range(HALVES)]
-        for h in range(HALVES):
-            for c in range(NT):
-                nc.scalar.activation(
-                    z_picked[h][:, c, :],
-                    tz_rows[c][:].indirect(list_z[:, h * LIST_COLS // HALVES : (h + 1) * LIST_COLS // HALVES]),
-                    COPY,
-                )
+        z_picked = [tile("z_picked_%d" % c, [P, J], F32) for c in range(NT)]
+        for c in range(NT):
+            gather(z_picked[c], tz_rows[c], list_z, 0, HALVES)
 
         pre = [tile("pre_%d" % h, [P, JH, PACK], BF16) for h in range(HALVES)]
         hid_woven = [tile("hid_woven_%d" % h, [P, JH, PACK], BF16) for h in range(HALVES)]
         hid_codes = [tile("hid_codes_%d" % h, [P, JH], U32) for h in range(HALVES)]
         hid_scale = [tile("hid_scale_%d" % h, [P, JH], U8) for h in range(HALVES)]
-        floored = [tile("floored_%d" % h, [P, NT, JH], F32) for h in range(HALVES)]
-        result = [tile("result_%d" % h, [P, NT, JH], F32) for h in range(HALVES)]
-        out_rows = out.rearrange("(c p) j -> p c j", p=P)
+        floored = [tile("floored_%d" % c, [P, J], F32) for c in range(NT)]
+        result = [tile("result_%d" % c, [P, J], F32) for c in range(NT)]
 
         def add_table(h):
             nc.vector.tensor_tensor(
@@ -343,7 +338,7 @@ def tile_list_centredpicks_tworeach_floored_kernel(
         def second_product(h):
             for c in range(NT):
                 nc.tensor.matmul_mx(
-                    out=p_acc[h][:, c, :],
+                    out=p_acc[c][:, h, :],
                     lhsT=wb_codes[:, c * P : (c + 1) * P].bitcast(E5M2X4),
                     lhsT_scale=wb_scale[:, c * P : (c + 1) * P],
                     rhs=hid_codes[h][:].bitcast(E5M2X4),
@@ -352,21 +347,23 @@ def tile_list_centredpicks_tworeach_floored_kernel(
                     stop=True,
                 )
 
-        def floor_by_table(h):
-            nc.vector.tensor_tensor(floored[h][:], p_acc[h][:], z_picked[h][:], ALU.max)
+        def floor_by_table(c):
+            nc.vector.tensor_tensor(floored[c][:], p_acc[c][:].rearrange("p h j -> p (h j)"), z_picked[c][:], ALU.max)
 
-        def weigh(h):
-            half_pairs = slice(h * JH // 2, (h + 1) * JH // 2)
+        def weigh(c):
             nc.vector.tensor_tensor(
-                result[h][:].rearrange("p c (m e) -> p c m e", e=2),
-                floored[h][:].rearrange("p c (m e) -> p c m e", e=2),
-                rw_all[:, :, half_pairs].rearrange("p e m -> p m e").unsqueeze(1).to_broadcast([P, NT, JH // 2, 2]),
+                result[c][:].rearrange("p (m e) -> p m e", e=2),
+                floored[c][:].rearrange("p (m e) -> p m e", e=2),
+                rw_all[:].rearrange("p e m -> p m e"),
                 ALU.mult,
             )
 
-        def store(h):
-            nc.sync.dma_start(out_rows[:, :, h * JH : (h + 1) * JH], result[h][:])
+        def store(c):
+            nc.sync.dma_start(out[c * P : (c + 1) * P, :], result[c][:])
 
-        for step in (add_table, relu_weave, quantise_hid, second_product, floor_by_table, weigh, store):
+        for step in (add_table, relu_weave, quantise_hid, second_product):
             for h in range(HALVES):
                 step(h)
+        for step in (floor_by_table, weigh, store):
+            for c in range(NT):
+                step(c)

from contextlib import ExitStack

import concourse.mybir as mybir
from concourse.masks import make_identity

K, T, J, R, V, N, Z = 1024, 1024, 256, 512, 512, 256, 512
GROUP = 8

F32 = mybir.dt.float32
BF16 = mybir.dt.bfloat16
I32 = mybir.dt.int32
U32 = mybir.dt.uint32
U16 = mybir.dt.uint16
U8 = mybir.dt.uint8
E4M3X4 = mybir.dt.float8_e4m3fn_x4
E5M2X4 = mybir.dt.float8_e5m2_x4
E2M1X4 = mybir.dt.float4_e2m1fn_x4
ALU = mybir.AluOpType
COPY = mybir.ActivationFunctionType.Copy

P = 128
PACK = 4
PASSES = K // (P * PACK)
HALVES = 2
JH = J // HALVES
LIST_COLS = J // 16
NT = N // P

FLOPS = 2 * K * R * J + 2 * R * N * J


def tile_list_centredpicks_tworeach_floored_kernel(
    tc, xf, fk, w_words, w_scales, tb, wb_words, wb_scales, tz, rw, offs, offs2, offs3, offs4, out
):
    nc = tc.nc
    with ExitStack() as ctx:
        sb = ctx.enter_context(tc.tile_pool(name="sb", bufs=1))
        ps = ctx.enter_context(tc.psum_pool(name="ps", bufs=1))

        def tile(name, shape, dtype):
            return sb.tile(shape, dtype, name=name, align_bytes=64)

        list_x = tile("list_x", [P, LIST_COLS], U16)
        list_add = tile("list_add", [P, LIST_COLS], U16)
        list_sub = tile("list_sub", [P, LIST_COLS], U16)
        list_z = tile("list_z", [P, LIST_COLS], U16)
        x_plane = [[tile("x_%d_%d" % (a, t), [P, T], F32) for t in range(PACK)] for a in range(PASSES)]
        tb_plane = [tile("tb_%d" % t, [P, V], F32) for t in range(PACK)]
        tz_rows = [tile("tz_%d" % c, [P, Z], F32) for c in range(NT)]
        fk_padded = tile("fk_padded", [P, PASSES, 2 * PACK], F32)
        fk_cols = fk_padded[:, :, :PACK]
        rw_pairs = tile("rw_pairs", [P, 2], F32)
        w_raw = tile("w_raw", [P, PASSES, 2 * R], U8)
        w_scale_raw = tile("w_scale_raw", [P, PASSES, R], U8)
        w_codes = tile("w_codes", [P, PASSES, 2 * R], U8)
        w_scale = tile("w_scale", [P, PASSES, R], U8)
        wb_codes = tile("wb_codes", [P, N], U32)
        wb_scale = tile("wb_scale", [P, N], U8)
        ident = tile("ident", [P, P], F32)

        nc.vector.memset(w_scale_raw[:].bitcast(U32), 0)
        nc.vector.memset(wb_scale[:].bitcast(U32), 0)
        warm = tile("warm", [P, 2], F32)
        nc.vector.memset(warm[:, 0:1], 0.0)

        x_rows = xf.rearrange("(a p t) c -> a t p c", p=P, t=PACK)
        tb_rows = tb.rearrange("(p t) c -> t p c", t=PACK)

        def load_x(i):
            a, t = divmod(i, PACK)
            nc.sync.dma_start(x_plane[a][t][:], x_rows[a, t])

        def load_tb(t):
            nc.sync.dma_start(tb_plane[t][:], tb_rows[t])

        def load_w_scale(q, queue=nc.sync):
            queue.dma_start(
                w_scale_raw[32 * q : 32 * q + 4].bitcast(I32),
                w_scales[:, 4 * q : 4 * q + 4, :].rearrange("a r c -> r a c").bitcast(I32),
            )

        def load_wb_scale(q):
            nc.sync.dma_start(wb_scale[32 * q : 32 * q + 4].bitcast(I32), wb_scales[0, 4 * q : 4 * q + 4, :].bitcast(I32))

        load_x(0)
        load_w_scale(0, nc.gpsimd)
        load_w_scale(1, nc.gpsimd)
        make_identity(nc, ident[:])
        nc.sync.dma_start(list_x[:], offs)
        nc.sync.dma_start(list_add[:], offs2)
        nc.sync.dma_start(list_sub[:], offs3)
        load_tb(3)
        nc.sync.dma_start(fk_cols[:], fk.rearrange("(a p t) o -> p a (t o)", p=P, t=PACK))
        load_x(1)
        load_x(2)
        load_w_scale(2)
        load_w_scale(3)
        load_x(3)
        load_x(4)
        load_x(5)
        load_x(6)
        load_tb(0)
        nc.sync.dma_start(w_raw[:].bitcast(I32), w_words.rearrange("a p c -> p a c").bitcast(I32))
        load_x(7)
        load_tb(1)
        load_tb(2)
        nc.sync.dma_start(list_z[:], offs4)
        nc.sync.dma_start(rw_pairs[:], rw.rearrange("o (p e) -> p (o e)", e=2))
        nc.sync.dma_start(tz_rows[0][:], tz[0 * P : (0 + 1) * P, :])
        nc.sync.dma_start(tz_rows[1][:], tz[1 * P : (1 + 1) * P, :])
        nc.sync.dma_start(wb_codes[:].bitcast(I32), wb_words[0].rearrange("p n t -> p (n t)").bitcast(I32))
        load_wb_scale(0)
        load_wb_scale(1)
        load_wb_scale(2)
        load_wb_scale(3)

        nc.scalar.activation(warm[:, 1:2], warm[:, 0:1], COPY)

        def gather(dst, window, offsets, h0, h1):
            nc.scalar.activation(
                dst[:, h0 * JH : h1 * JH],
                window[:].indirect(offsets[:, h0 * LIST_COLS // HALVES : h1 * LIST_COLS // HALVES]),
                COPY,
            )

        def gather_on_vector(dst, window, offsets, h0, h1):
            nc.vector.tensor_copy(
                dst[:, h0 * JH : h1 * JH],
                window[:].indirect(offsets[:, h0 * LIST_COLS // HALVES : h1 * LIST_COLS // HALVES]),
            )

        tb_diff = tile("tb_diff", [P, PACK, J], F32)
        picked = [
            [tb_diff[:, 3, :], tile("picked_0_1", [P, J], F32), tile("picked_0_2", [P, J], F32), tile("picked_0_3", [P, J], F32)],
            [tile("picked_1_0", [P, J], F32), tile("picked_1_1", [P, J], F32), tile("picked_1_2", [P, J], F32), tb_diff[:, 0, :]],
        ]
        means = [tile("means_%d" % a, [P, PACK, J // GROUP], F32) for a in range(PASSES)]
        u_planes = [
            tile("u_planes_0", [P, HALVES, PACK, JH], BF16),
            tb_diff[:, 1:3, :].bitcast(BF16).rearrange("p h (t j) -> p h t j", j=JH),
        ]
        spent = u_planes[0][:, HALVES - 1].bitcast(F32)
        sums = [
            [tile("sums_0_%d" % t, [P, J // GROUP], F32) for t in range(PACK)],
            [tile("sums_1_%d" % t, [P, J // GROUP], F32) for t in range(PACK)],
        ]
        u_woven = [tile("u_woven_%d" % a, [P, HALVES, JH, PACK], BF16) for a in range(PASSES)]
        u_codes = [tile("u_codes_%d" % a, [P, J], U32) for a in range(PASSES)]
        u_scale = [tile("u_scale_%d" % a, [P, J], U8) for a in range(PASSES)]
        tb_add = [tile("tb_add_%d" % t, [P, J], F32) for t in range(PACK)]
        tb_sub = [tile("tb_sub_%d" % t, [P, J], F32) for t in range(PACK)]
        a_acc = [ps.tile([P, PACK, JH], F32, name="a_acc_%d" % h) for h in range(HALVES)]
        p_acc = [ps.tile([P, HALVES, JH], F32, name="p_acc_%d" % c) for c in range(NT)]
        rw_all = ps.tile([P, 2, P], F32, name="rw_all")
        BH = JH // GROUP

        def group_sums(a, t, h0, h1):
            nc.vector.tensor_reduce(
                sums[a][t][:, h0 * BH : h1 * BH],
                picked[a][t][:, h0 * JH : h1 * JH].rearrange("p (b i) -> p b i", i=GROUP),
                mybir.AxisListType.X,
                ALU.add,
            )

        def group_means(a, t, h0, h1):
            nc.vector.tensor_scalar(
                means[a][:, t, h0 * BH : h1 * BH],
                sums[a][t][:, h0 * BH : h1 * BH],
                fk_cols[:, a, t : t + 1],
                1.0 / GROUP,
                ALU.mult,
                ALU.mult,
            )

        def centre(a, t, h0, h1):
            nh = h1 - h0
            nc.vector.scalar_tensor_tensor(
                u_planes[a][:, h0:h1, t, :].rearrange("p h (b i) -> p h b i", i=GROUP),
                picked[a][t][:, h0 * JH : h1 * JH].rearrange("p (h b i) -> p h b i", h=nh, i=GROUP),
                fk_cols[:, a, t : t + 1],
                means[a][:, t, h0 * BH : h1 * BH]
                .rearrange("p (h b) -> p h b", h=nh)
                .unsqueeze(3)
                .to_broadcast([P, nh, BH, GROUP]),
                ALU.mult,
                ALU.subtract,
            )

        def weave_u(a, h, copy=nc.vector.tensor_copy):
            copy(
                u_woven[a][:, h].rearrange("p (c i) t -> p c t i", i=4),
                u_planes[a][:, h].rearrange("p t (c i) -> p c t i", i=4),
            )

        def quantise_u(a, h):
            cols = slice(h * JH, (h + 1) * JH)
            nc.vector.quantize_mx(
                out=u_codes[a][:, cols].bitcast(E4M3X4),
                scales=u_scale[a][:, cols],
                in_=u_woven[a][:, h].rearrange("p j t -> p (j t)"),
            )

        def first_product(a, h):
            cols = slice(h * JH, (h + 1) * JH)
            for t in range(PACK):
                nc.tensor.matmul_mx(
                    out=a_acc[h][:, t, :],
                    lhsT=w_codes[:, a, 2 * P * t : 2 * P * (t + 1)].bitcast(E2M1X4),
                    lhsT_scale=w_scale[:, a, P * t : P * (t + 1)],
                    rhs=u_codes[a][:, cols].bitcast(E4M3X4),
                    rhs_scale=u_scale[a][:, cols],
                    start=(a == 0 and t == 0),
                    stop=(a == PASSES - 1 and t == PACK - 1),
                )

        def table_difference(t, h0, h1):
            cols = slice(h0 * JH, h1 * JH)
            nc.vector.tensor_tensor(
                tb_diff[:, t, cols],
                tb_add[t][:, cols],
                tb_sub[t][:, cols],
                ALU.subtract,
            )

        def pick_and_sum(a, t, gather=gather):
            gather(picked[a][t], x_plane[a][t], list_x, 0, HALVES)
            group_sums(a, t, 0, HALVES)

        def tb_whole(t):
            gather(tb_add[t], tb_plane[t], list_add, 0, HALVES)
            gather(tb_sub[t], tb_plane[t], list_sub, 0, HALVES)
            table_difference(t, 0, HALVES)

        def x_whole(a, t, gather=gather):
            pick_and_sum(a, t, gather)
            group_means(a, t, 0, HALVES)
            centre(a, t, 0, HALVES)

        x_whole(0, 0)
        fk_last = tile("fk_last", [P, JH], F32)
        nc.vector.tensor_copy(fk_last[:], fk_cols[:, PASSES - 1, PACK - 1 : PACK].to_broadcast([P, JH]))
        x_whole(0, 1)
        gather(tb_add[3], tb_plane[3], list_add, 0, HALVES)
        gather(tb_sub[3], tb_plane[3], list_sub, 0, HALVES)
        table_difference(3, 0, HALVES)
        for a in range(PASSES):
            nc.vector.tensor_copy(
                w_scale[:, a].rearrange("p (t b i) -> p b t i", t=PACK, i=16),
                w_scale_raw[:, a].rearrange("p (b i t) -> p b t i", t=PACK, i=16),
            )
        x_whole(0, 2)
        x_whole(0, 3)
        weave_u(0, 0)
        weave_u(0, 1, nc.scalar.copy)
        for h in range(HALVES):
            quantise_u(0, h)
        x_whole(1, 0)
        x_whole(1, 1)
        x_whole(1, 2)
        gather(tb_add[0], tb_plane[0], list_add, 0, HALVES)
        gather(tb_sub[0], tb_plane[0], list_sub, 0, HALVES)
        nc.vector.tensor_copy(
            w_codes[:, 0:1].bitcast(U16).rearrange("p a (t b i) -> p a b t i", t=PACK, i=8),
            w_raw[:, 0:1].bitcast(U16).rearrange("p a (b i t) -> p a b t i", t=PACK, i=8),
        )
        nc.vector.tensor_copy(
            w_codes[:, 1:2].bitcast(U16).rearrange("p a (t b i) -> p a b t i", t=PACK, i=8),
            w_raw[:, 1:2].bitcast(U16).rearrange("p a (b i t) -> p a b t i", t=PACK, i=8),
        )
        for h in range(HALVES):
            first_product(0, h)
        a, t = PASSES - 1, PACK - 1
        nc.vector.tensor_tensor(
            picked[a][t][:, :JH], x_plane[a][t][:].indirect(list_x[:, : LIST_COLS // HALVES]), fk_last[:], ALU.mult
        )
        gather(picked[a][t], x_plane[a][t], list_x, 1, 2)
        for h in range(HALVES):
            group_sums(a, t, h, h + 1)
        nc.vector.scalar_tensor_tensor(
            u_planes[a][:, 0, t, :].rearrange("p (b i) -> p b i", i=GROUP),
            sums[a][t][:, :BH].unsqueeze(2).to_broadcast([P, BH, GROUP]),
            -1.0 / GROUP,
            picked[a][t][:, :JH].rearrange("p (b i) -> p b i", i=GROUP),
            ALU.mult,
            ALU.add,
        )
        group_means(a, t, 1, 2)
        centre(a, t, 1, 2)
        for step in (weave_u, quantise_u):
            for h in range(HALVES):
                step(a, h)
        for h in range(HALVES):
            first_product(a, h)
        for h in range(HALVES):
            table_difference(0, h, h + 1)
            for t in (1, 2):
                gather(tb_add[t], tb_plane[t], list_add, h, h + 1)
                gather(tb_sub[t], tb_plane[t], list_sub, h, h + 1)
                table_difference(t, h, h + 1)

        for e in range(2):
            nc.tensor.transpose(rw_all[:, e, :], rw_pairs[:, e : e + 1].to_broadcast([P, P]), ident[:])
        z_picked = [tile("z_picked_%d" % c, [P, J], F32) for c in range(NT)]
        for c in range(NT):
            gather(z_picked[c], tz_rows[c], list_z, 0, HALVES)

        pre = [tile("pre_%d" % h, [P, JH, PACK], BF16) for h in range(HALVES)]
        hid_woven = [tile("hid_woven_%d" % h, [P, JH, PACK], BF16) for h in range(HALVES)]
        hid_codes = [tile("hid_codes_%d" % h, [P, JH], U32) for h in range(HALVES)]
        hid_scale = [tile("hid_scale_%d" % h, [P, JH], U8) for h in range(HALVES)]
        floored = [tile("floored_%d" % c, [P, J], F32) for c in range(NT)]
        result = [tile("result_%d" % c, [P, J], F32) for c in range(NT)]

        def add_table(h):
            nc.vector.tensor_tensor(
                pre[h][:].rearrange("p (c i) t -> p c t i", i=4),
                a_acc[h][:].rearrange("p t (c i) -> p c t i", i=4),
                tb_diff[:, :, h * JH : (h + 1) * JH].rearrange("p t (c i) -> p c t i", i=4),
                ALU.add,
            )

        def relu_weave(h):
            nc.vector.tensor_scalar(
                hid_woven[h][:],
                pre[h][:],
                0.0,
                None,
                ALU.max,
            )

        def quantise_hid(h):
            nc.vector.quantize_mx(
                out=hid_codes[h][:].bitcast(E5M2X4),
                scales=hid_scale[h][:],
                in_=hid_woven[h][:].rearrange("p j t -> p (j t)"),
            )

        def second_product(h):
            for c in range(NT):
                nc.tensor.matmul_mx(
                    out=p_acc[c][:, h, :],
                    lhsT=wb_codes[:, c * P : (c + 1) * P].bitcast(E5M2X4),
                    lhsT_scale=wb_scale[:, c * P : (c + 1) * P],
                    rhs=hid_codes[h][:].bitcast(E5M2X4),
                    rhs_scale=hid_scale[h][:],
                    start=True,
                    stop=True,
                )

        def floor_by_table(c):
            nc.vector.tensor_tensor(floored[c][:], p_acc[c][:].rearrange("p h j -> p (h j)"), z_picked[c][:], ALU.max)

        def weigh(c):
            nc.vector.tensor_tensor(
                result[c][:].rearrange("p (m e) -> p m e", e=2),
                floored[c][:].rearrange("p (m e) -> p m e", e=2),
                rw_all[:].rearrange("p e m -> p m e"),
                ALU.mult,
            )

        def store(c):
            nc.sync.dma_start(out[c * P : (c + 1) * P, :], result[c][:])

        for step in (add_table, relu_weave, quantise_hid, second_product):
            for h in range(HALVES):
                step(h)
        for step in (floor_by_table, weigh, store):
            for c in range(NT):
                step(c)
